import numpy as np, ml_dtypes
CORES = [2,3,6,7,58,59,62,63,114,115,118,119]
N = 12
NH, QP = 6, 64
def setup_inputs(rng):
    q = rng.standard_normal((N, 128, NH * QP), dtype=np.float32) / 4; k = rng.standard_normal((N, 128, NH * 128), dtype=np.float32)
    a = 2 * np.pi * rng.random((N, NH * QP)); s = 400 * rng.random((N, NH * QP)) ** 1.5; q[:, 0, :] = s * np.cos(a); q[:, 1, :] = s * np.sin(a); q[:, 2, :] = 150 * rng.standard_normal((N, NH * QP)); k[:, 2, :] = 1 + k[:, 2, :] / 50
    a = (2 * np.pi * rng.random((1, NH, 1)) + np.pi / 2 * (rng.permuted(np.tile(np.arange(N), (NH, 1)), axis=1).T.reshape(N, NH, 1) + 0.5) / N - 0.5 + rng.random((N, NH, 128))).reshape(N, NH * 128); k[:, 0, :] = np.cos(a); k[:, 1, :] = np.sin(a)
    return {"q": q.astype(ml_dtypes.bfloat16), "k": k.astype(ml_dtypes.bfloat16), "v": rng.standard_normal((N, 128, NH * 128), dtype=np.float32).astype(ml_dtypes.bfloat16)}
def setup_inputs_big(rng):
    d = setup_inputs(rng)
    for k in ("v",): d[k] = (d[k].astype(np.float32) * 1048576.0).astype(d[k].dtype)
    return d
def setup_inputs_small(rng):
    d = setup_inputs(rng)
    for k in ("v",): d[k] = (d[k].astype(np.float32) * (1 / 1048576.0)).astype(d[k].dtype)
    return d
def reference(q, k, v):
    Q, K, V = q.astype(np.float64), k.astype(np.float64), v.astype(np.float64)
    y = np.zeros((N, QP, NH * 128))
    for r in range(N):
        for h in range(NH):
            S = np.concatenate([K[j][:, 128 * h:128 * h + 128].T @ Q[r][:, QP * h:QP * h + QP] for j in range(N)], axis=0)
            P = np.exp(S - S.max(axis=0)); P = P / P.sum(axis=0)
            y[r][:, 128 * h:128 * h + 128] = P.T @ np.concatenate([V[j][:, 128 * h:128 * h + 128] for j in range(N)], axis=0)
    return {"y": y.astype(ml_dtypes.bfloat16)}

@@ -1,0 +1,327 @@
+from concourse.bass import DstId, RemoteDMATransfer
+from concourse.mybir import AluOpType, AxisListType, ActivationFunctionType
+
+NH, QP, KP, FD = 6, 64, 128, 128
+HH = NH // 2
+OW = FD + 8
+OCH = [(0, 1), (1, 2), (2, 3)]
+
+BF, F32 = "bfloat16", "float32"
+SCRATCH = {
+    "QOWN": ("sbuf", [128, NH * QP], BF),
+    "QL": ("sbuf", [128, 2 * NH * QP], BF),
+    "QK": ("sbuf", [128, NH * 2 * QP], BF),
+    "KB": ("sbuf", [128, 4 * NH * KP], BF),
+    "VB": ("sbuf", [128, 4 * NH * FD], BF),
+    "ONES": ("sbuf", [128, 128], BF),
+    "IDENT": ("sbuf", [128, 128], BF),
+    "NEGM": ("sbuf", [128, 8], BF),
+    "P0": ("sbuf", [128, 512], BF), "P1": ("sbuf", [128, 512], BF),
+    "PT0": ("sbuf", [128, 512], BF), "PT1": ("sbuf", [128, 512], BF),
+    "OA": ("sbuf", [128, 3 * OW], BF), "OC": ("sbuf", [128, 3 * OW], BF),
+    "LR0": ("sbuf", [128, 3 * OW], BF), "LR1": ("sbuf", [128, 3 * OW], BF),
+    "LW0": ("sbuf", [128, 3 * OW], BF), "LW1": ("sbuf", [128, 3 * OW], BF),
+    "ST": ("sbuf", [128, 24], F32), "NMIN": ("sbuf", [128, 4], F32), "W": ("sbuf", [128, 12], F32),
+    "WL": ("sbuf", [128, 12], F32), "LS": ("sbuf", [128, 4], F32), "RL": ("sbuf", [128, 4], F32),
+    "D": ("sbuf", [128, 2 * 4 * 128], BF),
+    "YS": ("sbuf", [128, 3 * FD], BF),
+    "S0": ("psum", [128, 512], F32), "S1": ("psum", [128, 512], F32),
+    "PTP0": ("psum", [128, 1024], BF), "PTP1": ("psum", [128, 1024], BF),
+    "O0": ("psum", [128, 512], F32), "O1": ("psum", [128, 512], F32),
+    "Y0": ("psum", [128, 512], F32), "Y1": ("psum", [128, 512], F32),
+}
+SEMAPHORES = ["s_pe", "s_ve", "s_ac", "s_gp", "ld_q", "ld_kv0", "ld_kv1", "qa", "kv0", "kv1",
+              "oa0", "oa1", "oa2", "wa", "ls", "st"]
+
+EQ, EKV, EQH, EKVH, EO, EW = 4, 8, 4, 4, 4, 8
+
+
+def _layout(T, topo):
+    ranks = list(T.cores)
+    chips = sorted({topo.chip(c) for c in ranks})
+    ncores = topo.CHIPS * topo.CORES_PER_CHIP
+    lay = {}
+    for ch in chips:
+        rs = [c for c in ranks if topo.chip(c) == ch]
+        order, helpers = [], []
+        for d in sorted({topo.die(c) for c in rs}):
+            order += sorted(c for c in rs if topo.die(c) == d)
+            helpers.append(sorted(c for c in range(ncores)
+                                  if topo.chip(c) == ch and topo.die(c) == d and c not in ranks)[:2])
+        lay[ch] = (order, helpers)
+    return chips, lay
+
+
+def rank_program(g, core, T, topo):
+    chips, lay = _layout(T, topo)
+    ch = topo.chip(core)
+    if ch not in lay:
+        return
+    order, helpers = lay[ch]
+    is_rank = core in order
+    hpos = [(p, hh) for p in range(len(helpers)) for hh in range(2) if helpers[p][hh] == core]
+    if not is_rank and not hpos:
+        return
+
+    Exp, Copy = ActivationFunctionType.Exp, ActivationFunctionType.Copy
+    QUE = {"pe": g.tensor, "ve": g.vector, "ac": g.scalar, "gp": g, "sy": g.sync}
+    ESEM = {"pe": "s_pe", "ve": "s_ve", "ac": "s_ac", "gp": "s_gp"}
+    cnt = {"s_pe": 0, "s_ve": 0, "s_ac": 0, "s_gp": 0, "ls": 0, "st": 0}
+    seen = {}
+
+    def done(e, ins):
+        name = ESEM[e]
+        ins.then_inc(T.sem[name], 1)
+        cnt[name] += 1
+        return (name, cnt[name])
+
+    def need(q, *toks):
+        for t in toks:
+            if t is None:
+                continue
+            name, n = t
+            if seen.get((q, name), 0) < n:
+                QUE[q].wait_ge(T.sem[name], n)
+                seen[(q, name)] = n
+
+    def engines(dsts):
+        m = -1
+        for d in dsts:
+            assert topo.may_write(core, d)
+            m &= topo.mask(core, d)
+        return [e for e in range(64) if (m >> e) & 1]
+
+    def xfer(src, dst_ap, dsts, engs, sem):
+        ids = []
+        for d in dsts:
+            rid, pid, _se = topo.addr(d)
+            ids.append(DstId(rid=rid, pnc=pid))
+        m = 0
+        for e in engs:
+            m |= 1 << e
+        cnt["ls"] += len(engs)
+        return RemoteDMATransfer(dst_ids=ids, dma_engine_mask=m, remote_sem=T.sem[sem], srcs=[src],
+                                 dsts=[dst_ap] * len(dsts), alu_op=0)
+
+    def fused(trs):
+        g.remote_dma_fused(trs, local_sem=T.sem.ls)
+
+    Sps, PTP, Ops, Yps = [T.S0, T.S1], [T.PTP0, T.PTP1], [T.O0, T.O1], [T.Y0, T.Y1]
+    Pb, PTb = [T.P0, T.P1], [T.PT0, T.PT1]
+
+    t_ones = done("ve", g.vector.memset(T.ONES[:, :], 1.0))
+    t_pad = done("ve", g.vector.memset(T.OA[:, :], 0.0))
+    if is_rank:
+        done("ve", g.vector.memset(T.OC[:, :], 0.0))
+        t_pad = done("ve", g.vector.memset(T.D[:, :], 0.0))
+    need("gp", t_ones)
+    t_id = done("gp", g.affine_select(T.IDENT[:, :], T.ONES[:, :], [[-1, 128]], AluOpType.is_equal, 0.0, 0, 1))
+
+    def run_units(units):
+        n = len(units)
+        tS, tMAX, tEXP, tT, tPTC, tPV, tEV = ([None] * n for _ in range(7))
+
+        def prev(lst, u):
+            return lst[u - 2] if u >= 2 else None
+
+        def stage_S(u):
+            h = units[u]["h"]
+            need("ve", units[u]["deps"][0])
+            for slot in range(2):
+                tq = done("ve", g.vector.tensor_copy(T.QK[:, (2 * h + slot) * QP:(2 * h + slot + 1) * QP],
+                                                     T.QL[:, (slot * NH + h) * QP:(slot * NH + h + 1) * QP]))
+            need("pe", tq, *units[u]["deps"])
+            need("pe", prev(tEXP, u), prev(tMAX, u))
+            for kb in range(4):
+                tS[u] = done("pe", g.tensor.matmul(Sps[u % 2][:, kb * 128:(kb + 1) * 128],
+                                                   T.QK[:, 2 * h * QP:(2 * h + 2) * QP],
+                                                   T.KB[:, kb * NH * KP + h * KP: kb * NH * KP + (h + 1) * KP],
+                                                   start=True, stop=True))
+
+        def stage_MAX(u):
+            need("ve", tS[u])
+            tMAX[u] = done("ve", g.vector.tensor_reduce(T.NEGM[:, u:u + 1], Sps[u % 2][:, :], AxisListType.X,
+                                                        AluOpType.max, negate=True))
+            need("ve", tMAX[u], t_pad)
+            units[u]["tneg"] = units[u]["negm"](u)
+
+        def stage_EXP(u):
+            need("ac", tMAX[u], prev(tT, u), prev(tEV, u))
+            tEXP[u] = done("ac", g.scalar.activation(Pb[u % 2][:, :], Sps[u % 2][:, :], Exp,
+                                                     bias=T.NEGM[:, u:u + 1], scale=1.0,
+                                                     accum_out=Ops[u % 2][:, FD:FD + 1]))
+
+        def stage_T(u):
+            need("pe", tEXP[u], prev(tPTC, u), t_id)
+            for kb in range(4):
+                tT[u] = done("pe", g.tensor.transpose(PTP[u % 2][:, kb * 128:(kb + 1) * 128],
+                                                      Pb[u % 2][:, kb * 128:(kb + 1) * 128], T.IDENT[:, :]))
+
+        def stage_PTC(u):
+            need("ve", tT[u], prev(tPV, u))
+            tPTC[u] = done("ve", g.vector.tensor_copy(PTb[u % 2][:, :], PTP[u % 2][:, 0:512]))
+
+        def stage_PV(u):
+            h = units[u]["h"]
+            need("pe", tPTC[u], prev(tEV, u), tEXP[u])
+            for kb in range(4):
+                tPV[u] = done("pe", g.tensor.matmul(Ops[u % 2][:, 0:FD], PTb[u % 2][:, kb * 128:(kb + 1) * 128],
+                                                    T.VB[:, kb * NH * FD + h * FD: kb * NH * FD + (h + 1) * FD],
+                                                    start=(kb == 0), stop=(kb == 3)))
+
+        def stage_EV(u):
+            need("ac", tPV[u], tEXP[u], t_pad)
+            tEV[u] = units[u]["evac"](u, Ops[u % 2])
+
+        for u in range(min(2, n)):
+            stage_S(u)
+            stage_MAX(u)
+            stage_EXP(u)
+        for u in range(n):
+            stage_T(u)
+            stage_PTC(u)
+            if u + 2 < n:
+                stage_S(u + 2)
+                stage_MAX(u + 2)
+            stage_PV(u)
+            stage_EV(u)
+            if u + 2 < n:
+                stage_EXP(u + 2)
+        return tEV, [units[u]["tneg"] for u in range(n)]
+
+    def finish():
+        for name in ("s_pe", "s_ve", "s_ac", "s_gp", "ls", "st"):
+            if cnt[name]:
+                need("gp", (name, cnt[name]))
+
+    if not is_rank:
+        pair, hh = hpos[0]
+        deps = [("qa", 2 * EQH), ("kv%d" % hh, 4 * 2 * EKVH)]
+
+        def ev_h(u, ps):
+            return done("ac", g.scalar.activation(T.OA[:, u * OW:u * OW + FD + 1], ps[:, 0:FD + 1], Copy))
+
+        def ng_h(u):
+            return done("ve", g.vector.tensor_copy(T.OA[:, u * OW + FD + 1:u * OW + FD + 2], T.NEGM[:, u:u + 1]))
+
+        tEV, tNG = run_units([{"h": HH * hh + gi, "deps": deps, "evac": ev_h, "negm": ng_h} for gi in range(HH)])
+        need("gp", tEV[-1], tNG[-1], t_pad)
+        two = [order[2 * pair], order[2 * pair + 1]]
+        fused([xfer(T.OA[:, :], T["LW%d" % hh][:, :], two, engines(two)[:EW], "wa")])
+        finish()
+        return
+
+    i = order.index(core)
+    pair, flip = i // 2, i % 2
+    ci = chips.index(ch)
+    nch = len(chips)
+    A = lay[chips[(ci + 1) % nch]][0][i]
+    C = lay[chips[(ci + 2) % nch]][0][i]
+    peers = [c for c in order if c != core]
+    kcol = i * NH * KP
+
+    g.sync.dma_start(T.QOWN[:, :], T.q[:, :]).then_inc(T.sem.ld_q, 16)
+    for half in range(2):
+        a, b = half * HH * KP, (half + 1) * HH * KP
+        g.sync.dma_start(T.KB[:, kcol + a:kcol + b], T.k[:, a:b]).then_inc(T.sem["ld_kv%d" % half], 16)
+        g.scalar.dma_start(T.VB[:, kcol + a:kcol + b], T.v[:, a:b]).then_inc(T.sem["ld_kv%d" % half], 16)
+
+    need("gp", ("ld_q", 16))
+    eo = engines([A, C])
+    fused([xfer(T.QOWN[:, :], T.QL[:, NH * QP:2 * NH * QP], [A], eo[0:EQ], "qa"),
+           xfer(T.QOWN[:, :], T.QL[:, 0:NH * QP], [C], eo[EQ:2 * EQ], "qa")])
+    ep = engines(peers)
+    for half in range(2):
+        a, b = kcol + half * HH * KP, kcol + (half + 1) * HH * KP
+        need("gp", ("ld_kv%d" % half, 32))
+        fused([xfer(T.KB[:, a:b], T.KB[:, a:b], peers, ep[0:EKV], "kv%d" % half),
+               xfer(T.VB[:, a:b], T.VB[:, a:b], peers, ep[EKV:2 * EKV], "kv%d" % half)])
+    myh = helpers[pair]
+    eh = engines(myh)
+    fused([xfer(T.QOWN[:, hh * HH * QP:(hh + 1) * HH * QP],
+                T.QL[:, ((flip ^ hh) * NH + hh * HH) * QP:((flip ^ hh) * NH + (hh + 1) * HH) * QP],
+                [myh[hh]], eh[len(eh) - (hh + 1) * EQH:len(eh) - hh * EQH], "qa") for hh in range(2)])
+    allh = [helpers[p][hh] for p in range(len(helpers)) for hh in range(2)]
+    ea = engines(allh)
+    trs = []
+    for hh in range(2):
+        a, b = kcol + hh * HH * KP, kcol + (hh + 1) * HH * KP
+        dst = [helpers[p][hh] for p in range(len(helpers))]
+        trs.append(xfer(T.KB[:, a:b], T.KB[:, a:b], dst, ea[(2 * hh) * EKVH:(2 * hh + 1) * EKVH], "kv%d" % hh))
+        trs.append(xfer(T.VB[:, a:b], T.VB[:, a:b], dst, ea[(2 * hh + 1) * EKVH:(2 * hh + 2) * EKVH], "kv%d" % hh))
+    fused(trs)
+
+    def where(h):
+        return ((h // HH) ^ flip) * 64, (h % HH) * OW
+
+    def ev_r(u, ps):
+        r0, c0 = where(u)
+        done("ac", g.scalar.activation(T.OA[r0:r0 + 64, c0:c0 + FD + 1], ps[0:64, 0:FD + 1], Copy))
+        return done("ac", g.scalar.activation(T.OC[r0:r0 + 64, c0:c0 + FD + 1], ps[64:128, 0:FD + 1], Copy))
+
+    def ng_r(u):
+        r0, c0 = where(u)
+        done("ve", g.vector.tensor_copy(T.OA[r0:r0 + 64, c0 + FD + 1:c0 + FD + 2], T.NEGM[0:64, u:u + 1]))
+        return done("ve", g.vector.tensor_copy(T.OC[r0:r0 + 64, c0 + FD + 1:c0 + FD + 2], T.NEGM[64:128, u:u + 1]))
+
+    units = []
+    for h in range(NH):
+        half = h // HH
+        units.append({"h": h, "evac": ev_r, "negm": ng_r,
+                      "deps": [("qa", 2 * EQ), ("ld_kv%d" % half, 32), ("kv%d" % half, 3 * 2 * EKV)]})
+    tEV, tNG = run_units(units)
+
+    chunk_of = {}
+    for k, (g0, g1) in enumerate(OCH):
+        for gi in range(g0, g1):
+            chunk_of[gi] = k
+        last = HH + g1 - 1
+        need("gp", tEV[last], tNG[last], t_pad)
+        fused([xfer(T.OA[:, g0 * OW:g1 * OW], T.LR1[:, g0 * OW:g1 * OW], [A], eo[0:EO], "oa%d" % k),
+               xfer(T.OC[:, g0 * OW:g1 * OW], T.LR0[:, g0 * OW:g1 * OW], [C], eo[EO:2 * EO], "oa%d" % k)])
+
+    LW = [T.LW0, T.LW1]
+    lw_lo, lw_hi = LW[0 ^ flip], LW[1 ^ flip]
+    tMM, tYE = [None] * HH, [None] * HH
+    for gi in range(HH):
+        c0, b, w0, d0 = gi * OW, gi * 8, gi * 4, (gi % 2) * 512
+        arr = [("wa", 2 * EW), ("oa%d" % chunk_of[gi], 2 * EO)]
+        need("ve", *arr)
+        s0, s1 = c0 + FD, c0 + FD + 2
+        done("ve", g.vector.tensor_copy(T.ST[0:64, b:b + 2], lw_lo[0:64, s0:s1]))
+        done("ve", g.vector.tensor_copy(T.ST[64:128, b:b + 2], lw_hi[64:128, s0:s1]))
+        done("ve", g.vector.tensor_copy(T.ST[:, b + 2:b + 4], T.LR0[:, s0:s1]))
+        t = done("ve", g.vector.tensor_copy(T.ST[:, b + 4:b + 6], T.LR1[:, s0:s1]))
+        need("ve", t)
+        t = done("ve", g.vector.tensor_reduce(T.NMIN[:, gi:gi + 1], T.ST[:, b + 1:b + 6:2], AxisListType.X,
+                                              AluOpType.min))
+        need("ac", t)
+        t = done("ac", g.scalar.activation(T.W[:, w0:w0 + 3], T.ST[:, b + 1:b + 6:2], Exp,
+                                           bias=T.NMIN[:, gi:gi + 1], scale=-1.0))
+        need("ve", t, t_id, t_pad, tMM[gi - 2] if gi >= 2 else None)
+        for blk, r0, r1, c in ((0, 0, 64, 0), (1, 64, 128, 0), (2, 0, 128, 1), (3, 0, 128, 2)):
+            td = done("ve", g.vector.tensor_scalar(T.D[r0:r1, d0 + blk * 128:d0 + (blk + 1) * 128],
+                                                   T.IDENT[r0:r1, :], T.W[r0:r1, w0 + c:w0 + c + 1], None,
+                                                   AluOpType.mult))
+        t = done("ve", g.vector.tensor_tensor(T.WL[:, w0:w0 + 3], T.W[:, w0:w0 + 3], T.ST[:, b:b + 5:2],
+                                              AluOpType.mult))
+        need("ve", t)
+        t = done("ve", g.vector.tensor_reduce(T.LS[:, gi:gi + 1], T.WL[:, w0:w0 + 3], AxisListType.X, AluOpType.add))
+        need("ve", t)
+        trl = done("ve", g.vector.reciprocal(T.RL[:, gi:gi + 1], T.LS[:, gi:gi + 1]))
+
+        need("pe", td, tYE[gi - 2] if gi >= 2 else None, *arr)
+        yp = Yps[gi % 2]
+        for blk, src in enumerate((lw_lo, lw_hi, T.LR0, T.LR1)):
+            tMM[gi] = done("pe", g.tensor.matmul(yp[:, 0:FD], T.D[:, d0 + blk * 128:d0 + (blk + 1) * 128],
+                                                 src[:, c0:c0 + FD], start=(blk == 0), stop=(blk == 3)))
+        need("ac", tMM[gi], trl)
+        tYE[gi] = done("ac", g.scalar.activation(T.YS[:, gi * FD:(gi + 1) * FD], yp[:, 0:FD], Copy,
+                                                 scale=T.RL[:, gi:gi + 1]))
+        for blk, q in ((0, "sy"), (1, "ac")):
+            h = HH * (blk ^ flip) + gi
+            need(q, tYE[gi])
+            QUE[q].dma_start(T.y[:, h * FD:(h + 1) * FD],
+                             T.YS[blk * 64:(blk + 1) * 64, gi * FD:(gi + 1) * FD]).then_inc(T.sem.st, 16)
+            cnt["st"] += 16
+    finish()

@@ -3,13 +3,16 @@ from concourse.mybir import AluOpType, AxisListType, ActivationFunctionType
 
 NH, QP, KP, FD = 6, 64, 128, 128
 HH = NH // 2
-OW = FD + 8
-OCH = [(0, 1), (1, 2), (2, 3)]
+HQ = HH * QP
+BW = (FD + 8, FD // 2 + 8)
+BF_ = (FD, FD // 2)
+BO = (0, FD + 8)
+MW = BW[0] + BW[1]
 
 BF, F32 = "bfloat16", "float32"
 SCRATCH = {
     "QOWN": ("sbuf", [128, NH * QP], BF),
-    "QL": ("sbuf", [128, 2 * NH * QP], BF),
+    "QL": ("sbuf", [128, 4 * HQ], BF),
     "QK": ("sbuf", [128, NH * 2 * QP], BF),
     "KB": ("sbuf", [128, 4 * NH * KP], BF),
     "VB": ("sbuf", [128, 4 * NH * FD], BF),
@@ -18,22 +21,21 @@ SCRATCH = {
     "NEGM": ("sbuf", [128, 8], BF),
     "P0": ("sbuf", [128, 512], BF), "P1": ("sbuf", [128, 512], BF),
     "PT0": ("sbuf", [128, 512], BF), "PT1": ("sbuf", [128, 512], BF),
-    "OA": ("sbuf", [128, 3 * OW], BF), "OC": ("sbuf", [128, 3 * OW], BF),
-    "LR0": ("sbuf", [128, 3 * OW], BF), "LR1": ("sbuf", [128, 3 * OW], BF),
-    "LW0": ("sbuf", [128, 3 * OW], BF), "LW1": ("sbuf", [128, 3 * OW], BF),
-    "ST": ("sbuf", [128, 24], F32), "NMIN": ("sbuf", [128, 4], F32), "W": ("sbuf", [128, 12], F32),
-    "WL": ("sbuf", [128, 12], F32), "LS": ("sbuf", [128, 4], F32), "RL": ("sbuf", [128, 4], F32),
-    "D": ("sbuf", [128, 2 * 4 * 128], BF),
-    "YS": ("sbuf", [128, 3 * FD], BF),
+    "OA": ("sbuf", [128, 4 * MW], BF),
+    "LT": ("sbuf", [128, 6 * MW], BF),
+    "ST": ("sbuf", [128, 32], F32), "NMIN": ("sbuf", [128, 4], F32), "W": ("sbuf", [128, 16], F32),
+    "WL": ("sbuf", [128, 16], F32), "LS": ("sbuf", [128, 4], F32), "RL": ("sbuf", [128, 4], F32),
+    "D": ("sbuf", [128, 2 * 3 * 128], BF),
+    "YS": ("sbuf", [128, 4 * FD], BF),
     "S0": ("psum", [128, 512], F32), "S1": ("psum", [128, 512], F32),
     "PTP0": ("psum", [128, 1024], BF), "PTP1": ("psum", [128, 1024], BF),
     "O0": ("psum", [128, 512], F32), "O1": ("psum", [128, 512], F32),
     "Y0": ("psum", [128, 512], F32), "Y1": ("psum", [128, 512], F32),
 }
-SEMAPHORES = ["s_pe", "s_ve", "s_ac", "s_gp", "ld_q", "ld_kv0", "ld_kv1", "qa", "kv0", "kv1",
-              "oa0", "oa1", "oa2", "wa", "ls", "st"]
+SEMAPHORES = ["s_pe", "s_ve", "s_ac", "s_gp", "ld_q", "ld_kv0", "ld_kv1", "qa0", "qa1", "kv0", "kv1",
+              "oa00", "oa01", "oa10", "oa11", "ls", "st"]
 
-EQ, EKV, EQH, EKVH, EO, EW = 4, 8, 4, 4, 4, 8
+EQ, EQH, EKV, EO = 4, 2, 4, 4
 
 
 def _layout(T, topo):
@@ -59,9 +61,10 @@ def rank_program(g, core, T, topo):
         return
     order, helpers = lay[ch]
     is_rank = core in order
-    hpos = [(p, hh) for p in range(len(helpers)) for hh in range(2) if helpers[p][hh] == core]
+    hpos = [(p, x) for p in range(len(helpers)) for x in range(2) if helpers[p][x] == core]
     if not is_rank and not hpos:
         return
+    ci, nch = chips.index(ch), len(chips)
 
     Exp, Copy = ActivationFunctionType.Exp, ActivationFunctionType.Copy
     QUE = {"pe": g.tensor, "ve": g.vector, "ac": g.scalar, "gp": g, "sy": g.sync}
@@ -109,219 +112,220 @@ def rank_program(g, core, T, topo):
     Sps, PTP, Ops, Yps = [T.S0, T.S1], [T.PTP0, T.PTP1], [T.O0, T.O1], [T.Y0, T.Y1]
     Pb, PTb = [T.P0, T.P1], [T.PT0, T.PT1]
 
-    t_ones = done("ve", g.vector.memset(T.ONES[:, :], 1.0))
-    t_pad = done("ve", g.vector.memset(T.OA[:, :], 0.0))
     if is_rank:
-        done("ve", g.vector.memset(T.OC[:, :], 0.0))
-        t_pad = done("ve", g.vector.memset(T.D[:, :], 0.0))
+        i = order.index(core)
+        pair, pos = i // 2, i % 2
+        hh = pos
+        kcol = i * NH * KP
+        g.sync.dma_start(T.QOWN[:, :], T.q[:, :]).then_inc(T.sem.ld_q, 16)
+        for half in range(2):
+            a, b = half * HH * KP, (half + 1) * HH * KP
+            g.sync.dma_start(T.KB[:, kcol + a:kcol + b], T.k[:, a:b]).then_inc(T.sem["ld_kv%d" % half], 16)
+            g.scalar.dma_start(T.VB[:, kcol + a:kcol + b], T.v[:, a:b]).then_inc(T.sem["ld_kv%d" % half], 16)
+        jobs = [(lay[chips[(ci + 1) % nch]][0][2 * pair:2 * pair + 2], 2),
+                (lay[chips[(ci + 2) % nch]][0][2 * pair:2 * pair + 2], 1)]
+        kvdeps = [("ld_kv%d" % hh, 32), ("kv%d" % hh, 3 * 2 * EKV)]
+        units = [(0, 0), (1, 0), (0, 1), (1, 1), (2, 0), (2, 1)]
+        qcount = 2 * EQ
+    else:
+        pair, hh = hpos[0]
+        jobs = [(order[2 * pair:2 * pair + 2], 0)]
+        kvdeps = [("kv%d" % hh, 4 * 2 * EKV)]
+        units = [(2, 0), (0, 0), (1, 0)]
+        qcount = 2 * EQH
+
+    t_pad = done("ve", g.vector.memset(T.OA[:, :], 0.0))
+    need("ac", t_pad)
+    t_ones = done("ac", g.scalar.activation(T.ONES[:, :], T.OA[:, 0:128], Exp))
+
+    if is_rank:
+        eo = engines([lay[chips[(ci + s) % nch]][0][2 * pair + x] for s in (1, 2) for x in range(2)])
+
+        def q_far(s, jb):
+            trs = []
+            for x in range(2):
+                dst = lay[chips[(ci + s) % nch]][0][2 * pair + x]
+                c0 = (jb * 2 + pos) * HQ
+                trs.append(xfer(T.QOWN[:, x * HQ:(x + 1) * HQ], T.QL[:, c0:c0 + HQ], [dst],
+                                eo[x * EQ:(x + 1) * EQ], "qa%d" % jb))
+            fused(trs)
+
+        def kv_out(to_ranks):
+            trs = []
+            for x in range(2):
+                a, b = kcol + x * HH * KP, kcol + (x + 1) * HH * KP
+                if to_ranks:
+                    dst = [order[2 * p + x] for p in range(len(helpers)) if order[2 * p + x] != core]
+                    ea = engines(dst)
+                    grp = [e for e in ea if (e in eo) == (x == pos)]
+                else:
+                    dst = [helpers[p][x] for p in range(len(helpers))]
+                    grp = engines(dst)[2 * x * EKV:(2 * x + 2) * EKV]
+                trs.append(xfer(T.KB[:, a:b], T.KB[:, a:b], dst, grp[0:EKV], "kv%d" % x))
+                trs.append(xfer(T.VB[:, a:b], T.VB[:, a:b], dst, grp[EKV:2 * EKV], "kv%d" % x))
+            fused(trs)
+
+        need("gp", ("ld_q", 16))
+        q_far(2, 0)
+        need("gp", ("ld_kv0", 32), ("ld_kv1", 32))
+        kv_out(True)
+        q_far(1, 1)
+        myh = helpers[pair]
+        eh = engines(myh)
+        fused([xfer(T.QOWN[:, x * HQ:(x + 1) * HQ], T.QL[:, pos * HQ:(pos + 1) * HQ],
+                    [myh[x]], eh[len(eh) - (x + 1) * EQH:len(eh) - x * EQH], "qa0") for x in range(2)])
+        kv_out(False)
+
     need("gp", t_ones)
     t_id = done("gp", g.affine_select(T.IDENT[:, :], T.ONES[:, :], [[-1, 128]], AluOpType.is_equal, 0.0, 0, 1))
 
-    def run_units(units):
-        n = len(units)
-        tS, tMAX, tEXP, tT, tPTC, tPV, tEV = ([None] * n for _ in range(7))
+    n = len(units)
+    tS, tMAX, tNG, tEXP, tT, tPTC, tPV, tEV = ([None] * n for _ in range(8))
 
-        def prev(lst, u):
-            return lst[u - 2] if u >= 2 else None
+    def prev(lst, u):
+        return lst[u - 2] if u >= 2 else None
 
-        def stage_S(u):
-            h = units[u]["h"]
-            need("ve", units[u]["deps"][0])
-            for slot in range(2):
-                tq = done("ve", g.vector.tensor_copy(T.QK[:, (2 * h + slot) * QP:(2 * h + slot + 1) * QP],
-                                                     T.QL[:, (slot * NH + h) * QP:(slot * NH + h + 1) * QP]))
-            need("pe", tq, *units[u]["deps"])
-            need("pe", prev(tEXP, u), prev(tMAX, u))
-            for kb in range(4):
-                tS[u] = done("pe", g.tensor.matmul(Sps[u % 2][:, kb * 128:(kb + 1) * 128],
-                                                   T.QK[:, 2 * h * QP:(2 * h + 2) * QP],
-                                                   T.KB[:, kb * NH * KP + h * KP: kb * NH * KP + (h + 1) * KP],
-                                                   start=True, stop=True))
+    def stage_S(u):
+        gi, jb = units[u]
+        h = HH * hh + gi
+        tqa = ("qa%d" % jb, qcount)
+        need("ve", tqa)
+        for slot in range(2):
+            c0 = (jb * 2 + slot) * HQ + gi * QP
+            tq = done("ve", g.vector.tensor_copy(T.QK[:, (2 * u + slot) * QP:(2 * u + slot + 1) * QP],
+                                                 T.QL[:, c0:c0 + QP]))
+        need("pe", tq, tqa, *kvdeps)
+        need("pe", prev(tEXP, u), prev(tMAX, u))
+        for kb in range(4):
+            tS[u] = done("pe", g.tensor.matmul(Sps[u % 2][:, kb * 128:(kb + 1) * 128],
+                                               T.QK[:, 2 * u * QP:(2 * u + 2) * QP],
+                                               T.KB[:, kb * NH * KP + h * KP: kb * NH * KP + (h + 1) * KP],
+                                               start=True, stop=True))
 
-        def stage_MAX(u):
-            need("ve", tS[u])
-            tMAX[u] = done("ve", g.vector.tensor_reduce(T.NEGM[:, u:u + 1], Sps[u % 2][:, :], AxisListType.X,
-                                                        AluOpType.max, negate=True))
-            need("ve", tMAX[u], t_pad)
-            units[u]["tneg"] = units[u]["negm"](u)
+    def stage_MAX(u):
+        gi, jb = units[u]
+        need("ve", tS[u])
+        tMAX[u] = done("ve", g.vector.tensor_reduce(T.NEGM[:, u:u + 1], Sps[u % 2][:, :], AxisListType.X,
+                                                    AluOpType.max, negate=True))
+        need("ve", tMAX[u], t_pad)
+        for x in range(2):
+            base, src = (jb * 2 + x) * MW, T.NEGM[x * 64:(x + 1) * 64, u:u + 1]
+            if gi < 2:
+                c0 = base + FD + 1
+                tNG[u] = done("ve", g.vector.tensor_copy(T.OA[gi * 64:(gi + 1) * 64, c0:c0 + 1], src))
+            else:
+                c0 = base + BO[1] + BF_[1] + 1
+                done("ve", g.vector.tensor_copy(T.OA[0:64, c0:c0 + 1], src))
+                tNG[u] = done("ve", g.vector.tensor_copy(T.OA[64:128, c0:c0 + 1], src))
 
-        def stage_EXP(u):
-            need("ac", tMAX[u], prev(tT, u), prev(tEV, u))
-            tEXP[u] = done("ac", g.scalar.activation(Pb[u % 2][:, :], Sps[u % 2][:, :], Exp,
-                                                     bias=T.NEGM[:, u:u + 1], scale=1.0,
-                                                     accum_out=Ops[u % 2][:, FD:FD + 1]))
+    def stage_EXP(u):
+        need("ac", tMAX[u], prev(tT, u), prev(tEV, u))
+        tEXP[u] = done("ac", g.scalar.activation(Pb[u % 2][:, :], Sps[u % 2][:, :], Exp,
+                                                 bias=T.NEGM[:, u:u + 1], scale=1.0,
+                                                 accum_out=Ops[u % 2][:, FD:FD + 1]))
 
-        def stage_T(u):
-            need("pe", tEXP[u], prev(tPTC, u), t_id)
-            for kb in range(4):
-                tT[u] = done("pe", g.tensor.transpose(PTP[u % 2][:, kb * 128:(kb + 1) * 128],
-                                                      Pb[u % 2][:, kb * 128:(kb + 1) * 128], T.IDENT[:, :]))
+    def stage_T(u):
+        need("pe", tEXP[u], prev(tPTC, u), t_id)
+        for kb in range(4):
+            tT[u] = done("pe", g.tensor.transpose(PTP[u % 2][:, kb * 128:(kb + 1) * 128],
+                                                  Pb[u % 2][:, kb * 128:(kb + 1) * 128], T.IDENT[:, :]))
 
-        def stage_PTC(u):
-            need("ve", tT[u], prev(tPV, u))
-            tPTC[u] = done("ve", g.vector.tensor_copy(PTb[u % 2][:, :], PTP[u % 2][:, 0:512]))
+    def stage_PTC(u):
+        need("ve", tT[u], prev(tPV, u))
+        tPTC[u] = done("ve", g.vector.tensor_copy(PTb[u % 2][:, :], PTP[u % 2][:, 0:512]))
 
-        def stage_PV(u):
-            h = units[u]["h"]
-            need("pe", tPTC[u], prev(tEV, u), tEXP[u])
-            for kb in range(4):
-                tPV[u] = done("pe", g.tensor.matmul(Ops[u % 2][:, 0:FD], PTb[u % 2][:, kb * 128:(kb + 1) * 128],
-                                                    T.VB[:, kb * NH * FD + h * FD: kb * NH * FD + (h + 1) * FD],
-                                                    start=(kb == 0), stop=(kb == 3)))
+    def stage_PV(u):
+        h = HH * hh + units[u][0]
+        need("pe", tPTC[u], prev(tEV, u), tEXP[u])
+        for kb in range(4):
+            tPV[u] = done("pe", g.tensor.matmul(Ops[u % 2][:, 0:FD], PTb[u % 2][:, kb * 128:(kb + 1) * 128],
+                                                T.VB[:, kb * NH * FD + h * FD: kb * NH * FD + (h + 1) * FD],
+                                                start=(kb == 0), stop=(kb == 3)))
 
-        def stage_EV(u):
-            need("ac", tPV[u], tEXP[u], t_pad)
-            tEV[u] = units[u]["evac"](u, Ops[u % 2])
+    def stage_EV(u):
+        gi, jb = units[u]
+        ps = Ops[u % 2]
+        need("ac", tPV[u], tEXP[u], t_pad, t_ones)
+        for x in range(2):
+            base, r0, r1 = (jb * 2 + x) * MW, x * 64, (x + 1) * 64
+            if gi < 2:
+                tEV[u] = done("ac", g.scalar.activation(T.OA[gi * 64:(gi + 1) * 64, base:base + FD + 1],
+                                                        ps[r0:r1, 0:FD + 1], Copy))
+            else:
+                c0, hf = base + BO[1], BF_[1]
+                done("ac", g.scalar.activation(T.OA[0:64, c0:c0 + hf], ps[r0:r1, 0:hf], Copy))
+                done("ac", g.scalar.activation(T.OA[0:64, c0 + hf:c0 + hf + 1], ps[r0:r1, FD:FD + 1], Copy))
+                tEV[u] = done("ac", g.scalar.activation(T.OA[64:128, c0:c0 + hf + 1], ps[r0:r1, hf:FD + 1], Copy))
 
-        for u in range(min(2, n)):
-            stage_S(u)
-            stage_MAX(u)
-            stage_EXP(u)
-        for u in range(n):
-            stage_T(u)
-            stage_PTC(u)
-            if u + 2 < n:
-                stage_S(u + 2)
-                stage_MAX(u + 2)
-            stage_PV(u)
-            stage_EV(u)
-            if u + 2 < n:
-                stage_EXP(u + 2)
-        return tEV, [units[u]["tneg"] for u in range(n)]
+    for u in range(min(2, n)):
+        stage_S(u)
+        stage_MAX(u)
+        stage_EXP(u)
+    for u in range(n):
+        stage_T(u)
+        stage_PTC(u)
+        if u + 2 < n:
+            stage_S(u + 2)
+            stage_MAX(u + 2)
+        stage_PV(u)
+        stage_EV(u)
+        if u + 2 < n:
+            stage_EXP(u + 2)
 
-    def finish():
-        for name in ("s_pe", "s_ve", "s_ac", "s_gp", "ls", "st"):
-            if cnt[name]:
-                need("gp", (name, cnt[name]))
+    for u in range(n):
+        gi, jb = units[u]
+        if gi == 0:
+            continue
+        blk = gi - 1
+        two, place = jobs[jb]
+        es = engines(two)
+        need("gp", tEV[u], tNG[u], t_pad)
+        fused([xfer(T.OA[:, (jb * 2 + x) * MW + BO[blk]:(jb * 2 + x) * MW + BO[blk] + BW[blk]],
+                    T.LT[:, (place * 2 + hh) * MW + BO[blk]:(place * 2 + hh) * MW + BO[blk] + BW[blk]],
+                    [two[x]], es[x * EO:(x + 1) * EO], "oa%d%d" % (hh, blk)) for x in range(2)])
 
-    if not is_rank:
-        pair, hh = hpos[0]
-        deps = [("qa", 2 * EQH), ("kv%d" % hh, 4 * 2 * EKVH)]
+    if is_rank:
+        combos = [(0, 0), (1, 0), (0, 1), (1, 1)]
+        tMM, tYE = [None] * 4, [None] * 4
+        for k, (hx, blk) in enumerate(combos):
+            b, w0, d0, fw = k * 8, k * 4, (k % 2) * 384, BF_[blk]
+            arr = ("oa%d%d" % (hx, blk), 3 * EO)
+            cols = [(c * 2 + hx) * MW + BO[blk] for c in range(3)]
+            need("ve", arr)
+            for c in range(3):
+                t = done("ve", g.vector.tensor_copy(T.ST[:, b + 2 * c:b + 2 * c + 2],
+                                                    T.LT[:, cols[c] + fw:cols[c] + fw + 2]))
+            need("ve", t)
+            sums, negs = T.ST[:, b:b + 5:2], T.ST[:, b + 1:b + 6:2]
+            t = done("ve", g.vector.tensor_reduce(T.NMIN[:, k:k + 1], negs, AxisListType.X, AluOpType.min))
+            need("ac", t)
+            t = done("ac", g.scalar.activation(T.W[:, w0:w0 + 3], negs, Exp, bias=T.NMIN[:, k:k + 1], scale=-1.0))
+            need("ve", t, t_id, tMM[k - 2] if k >= 2 else None)
+            for c in range(3):
+                td = done("ve", g.vector.tensor_scalar(T.D[:, d0 + c * 128:d0 + (c + 1) * 128], T.IDENT[:, :],
+                                                       T.W[:, w0 + c:w0 + c + 1], None, AluOpType.mult))
+            t = done("ve", g.vector.tensor_tensor(T.WL[:, w0:w0 + 3], T.W[:, w0:w0 + 3], sums, AluOpType.mult))
+            need("ve", t)
+            t = done("ve", g.vector.tensor_reduce(T.LS[:, k:k + 1], T.WL[:, w0:w0 + 3], AxisListType.X,
+                                                  AluOpType.add))
+            need("ve", t)
+            trl = done("ve", g.vector.reciprocal(T.RL[:, k:k + 1], T.LS[:, k:k + 1]))
 
-        def ev_h(u, ps):
-            return done("ac", g.scalar.activation(T.OA[:, u * OW:u * OW + FD + 1], ps[:, 0:FD + 1], Copy))
+            need("pe", td, arr, tYE[k - 2] if k >= 2 else None)
+            yp = Yps[k % 2]
+            for c in range(3):
+                tMM[k] = done("pe", g.tensor.matmul(yp[:, 0:fw], T.D[:, d0 + c * 128:d0 + (c + 1) * 128],
+                                                    T.LT[:, cols[c]:cols[c] + fw], start=(c == 0), stop=(c == 2)))
+            need("ac", tMM[k], trl)
+            tYE[k] = done("ac", g.scalar.activation(T.YS[:, k * FD:k * FD + fw], yp[:, 0:fw], Copy,
+                                                    scale=T.RL[:, k:k + 1]))
+            for lo, q in ((0, "sy"), (1, "ac")):
+                y0 = (HH * hx + lo) * FD if blk == 0 else (HH * hx + 2) * FD + lo * fw
+                need(q, tYE[k])
+                QUE[q].dma_start(T.y[:, y0:y0 + fw],
+                                 T.YS[lo * 64:(lo + 1) * 64, k * FD:k * FD + fw]).then_inc(T.sem.st, 16)
+                cnt["st"] += 16
 
-        def ng_h(u):
-            return done("ve", g.vector.tensor_copy(T.OA[:, u * OW + FD + 1:u * OW + FD + 2], T.NEGM[:, u:u + 1]))
-
-        tEV, tNG = run_units([{"h": HH * hh + gi, "deps": deps, "evac": ev_h, "negm": ng_h} for gi in range(HH)])
-        need("gp", tEV[-1], tNG[-1], t_pad)
-        two = [order[2 * pair], order[2 * pair + 1]]
-        fused([xfer(T.OA[:, :], T["LW%d" % hh][:, :], two, engines(two)[:EW], "wa")])
-        finish()
-        return
-
-    i = order.index(core)
-    pair, flip = i // 2, i % 2
-    ci = chips.index(ch)
-    nch = len(chips)
-    A = lay[chips[(ci + 1) % nch]][0][i]
-    C = lay[chips[(ci + 2) % nch]][0][i]
-    peers = [c for c in order if c != core]
-    kcol = i * NH * KP
-
-    g.sync.dma_start(T.QOWN[:, :], T.q[:, :]).then_inc(T.sem.ld_q, 16)
-    for half in range(2):
-        a, b = half * HH * KP, (half + 1) * HH * KP
-        g.sync.dma_start(T.KB[:, kcol + a:kcol + b], T.k[:, a:b]).then_inc(T.sem["ld_kv%d" % half], 16)
-        g.scalar.dma_start(T.VB[:, kcol + a:kcol + b], T.v[:, a:b]).then_inc(T.sem["ld_kv%d" % half], 16)
-
-    need("gp", ("ld_q", 16))
-    eo = engines([A, C])
-    fused([xfer(T.QOWN[:, :], T.QL[:, NH * QP:2 * NH * QP], [A], eo[0:EQ], "qa"),
-           xfer(T.QOWN[:, :], T.QL[:, 0:NH * QP], [C], eo[EQ:2 * EQ], "qa")])
-    ep = engines(peers)
-    for half in range(2):
-        a, b = kcol + half * HH * KP, kcol + (half + 1) * HH * KP
-        need("gp", ("ld_kv%d" % half, 32))
-        fused([xfer(T.KB[:, a:b], T.KB[:, a:b], peers, ep[0:EKV], "kv%d" % half),
-               xfer(T.VB[:, a:b], T.VB[:, a:b], peers, ep[EKV:2 * EKV], "kv%d" % half)])
-    myh = helpers[pair]
-    eh = engines(myh)
-    fused([xfer(T.QOWN[:, hh * HH * QP:(hh + 1) * HH * QP],
-                T.QL[:, ((flip ^ hh) * NH + hh * HH) * QP:((flip ^ hh) * NH + (hh + 1) * HH) * QP],
-                [myh[hh]], eh[len(eh) - (hh + 1) * EQH:len(eh) - hh * EQH], "qa") for hh in range(2)])
-    allh = [helpers[p][hh] for p in range(len(helpers)) for hh in range(2)]
-    ea = engines(allh)
-    trs = []
-    for hh in range(2):
-        a, b = kcol + hh * HH * KP, kcol + (hh + 1) * HH * KP
-        dst = [helpers[p][hh] for p in range(len(helpers))]
-        trs.append(xfer(T.KB[:, a:b], T.KB[:, a:b], dst, ea[(2 * hh) * EKVH:(2 * hh + 1) * EKVH], "kv%d" % hh))
-        trs.append(xfer(T.VB[:, a:b], T.VB[:, a:b], dst, ea[(2 * hh + 1) * EKVH:(2 * hh + 2) * EKVH], "kv%d" % hh))
-    fused(trs)
-
-    def where(h):
-        return ((h // HH) ^ flip) * 64, (h % HH) * OW
-
-    def ev_r(u, ps):
-        r0, c0 = where(u)
-        done("ac", g.scalar.activation(T.OA[r0:r0 + 64, c0:c0 + FD + 1], ps[0:64, 0:FD + 1], Copy))
-        return done("ac", g.scalar.activation(T.OC[r0:r0 + 64, c0:c0 + FD + 1], ps[64:128, 0:FD + 1], Copy))
-
-    def ng_r(u):
-        r0, c0 = where(u)
-        done("ve", g.vector.tensor_copy(T.OA[r0:r0 + 64, c0 + FD + 1:c0 + FD + 2], T.NEGM[0:64, u:u + 1]))
-        return done("ve", g.vector.tensor_copy(T.OC[r0:r0 + 64, c0 + FD + 1:c0 + FD + 2], T.NEGM[64:128, u:u + 1]))
-
-    units = []
-    for h in range(NH):
-        half = h // HH
-        units.append({"h": h, "evac": ev_r, "negm": ng_r,
-                      "deps": [("qa", 2 * EQ), ("ld_kv%d" % half, 32), ("kv%d" % half, 3 * 2 * EKV)]})
-    tEV, tNG = run_units(units)
-
-    chunk_of = {}
-    for k, (g0, g1) in enumerate(OCH):
-        for gi in range(g0, g1):
-            chunk_of[gi] = k
-        last = HH + g1 - 1
-        need("gp", tEV[last], tNG[last], t_pad)
-        fused([xfer(T.OA[:, g0 * OW:g1 * OW], T.LR1[:, g0 * OW:g1 * OW], [A], eo[0:EO], "oa%d" % k),
-               xfer(T.OC[:, g0 * OW:g1 * OW], T.LR0[:, g0 * OW:g1 * OW], [C], eo[EO:2 * EO], "oa%d" % k)])
-
-    LW = [T.LW0, T.LW1]
-    lw_lo, lw_hi = LW[0 ^ flip], LW[1 ^ flip]
-    tMM, tYE = [None] * HH, [None] * HH
-    for gi in range(HH):
-        c0, b, w0, d0 = gi * OW, gi * 8, gi * 4, (gi % 2) * 512
-        arr = [("wa", 2 * EW), ("oa%d" % chunk_of[gi], 2 * EO)]
-        need("ve", *arr)
-        s0, s1 = c0 + FD, c0 + FD + 2
-        done("ve", g.vector.tensor_copy(T.ST[0:64, b:b + 2], lw_lo[0:64, s0:s1]))
-        done("ve", g.vector.tensor_copy(T.ST[64:128, b:b + 2], lw_hi[64:128, s0:s1]))
-        done("ve", g.vector.tensor_copy(T.ST[:, b + 2:b + 4], T.LR0[:, s0:s1]))
-        t = done("ve", g.vector.tensor_copy(T.ST[:, b + 4:b + 6], T.LR1[:, s0:s1]))
-        need("ve", t)
-        t = done("ve", g.vector.tensor_reduce(T.NMIN[:, gi:gi + 1], T.ST[:, b + 1:b + 6:2], AxisListType.X,
-                                              AluOpType.min))
-        need("ac", t)
-        t = done("ac", g.scalar.activation(T.W[:, w0:w0 + 3], T.ST[:, b + 1:b + 6:2], Exp,
-                                           bias=T.NMIN[:, gi:gi + 1], scale=-1.0))
-        need("ve", t, t_id, t_pad, tMM[gi - 2] if gi >= 2 else None)
-        for blk, r0, r1, c in ((0, 0, 64, 0), (1, 64, 128, 0), (2, 0, 128, 1), (3, 0, 128, 2)):
-            td = done("ve", g.vector.tensor_scalar(T.D[r0:r1, d0 + blk * 128:d0 + (blk + 1) * 128],
-                                                   T.IDENT[r0:r1, :], T.W[r0:r1, w0 + c:w0 + c + 1], None,
-                                                   AluOpType.mult))
-        t = done("ve", g.vector.tensor_tensor(T.WL[:, w0:w0 + 3], T.W[:, w0:w0 + 3], T.ST[:, b:b + 5:2],
-                                              AluOpType.mult))
-        need("ve", t)
-        t = done("ve", g.vector.tensor_reduce(T.LS[:, gi:gi + 1], T.WL[:, w0:w0 + 3], AxisListType.X, AluOpType.add))
-        need("ve", t)
-        trl = done("ve", g.vector.reciprocal(T.RL[:, gi:gi + 1], T.LS[:, gi:gi + 1]))
-
-        need("pe", td, tYE[gi - 2] if gi >= 2 else None, *arr)
-        yp = Yps[gi % 2]
-        for blk, src in enumerate((lw_lo, lw_hi, T.LR0, T.LR1)):
-            tMM[gi] = done("pe", g.tensor.matmul(yp[:, 0:FD], T.D[:, d0 + blk * 128:d0 + (blk + 1) * 128],
-                                                 src[:, c0:c0 + FD], start=(blk == 0), stop=(blk == 3)))
-        need("ac", tMM[gi], trl)
-        tYE[gi] = done("ac", g.scalar.activation(T.YS[:, gi * FD:(gi + 1) * FD], yp[:, 0:FD], Copy,
-                                                 scale=T.RL[:, gi:gi + 1]))
-        for blk, q in ((0, "sy"), (1, "ac")):
-            h = HH * (blk ^ flip) + gi
-            need(q, tYE[gi])
-            QUE[q].dma_start(T.y[:, h * FD:(h + 1) * FD],
-                             T.YS[blk * 64:(blk + 1) * 64, gi * FD:(gi + 1) * FD]).then_inc(T.sem.st, 16)
-            cnt["st"] += 16
-    finish()
+    for name in ("s_pe", "s_ve", "s_ac", "s_gp", "ls", "st"):
+        if cnt[name]:
+            need("gp", (name, cnt[name]))

@@ -19,11 +19,12 @@ SCRATCH = {
     "ONES": ("sbuf", [128, 128], BF),
     "IDENT": ("sbuf", [128, 128], BF),
     "NEGM": ("sbuf", [128, 8], BF),
+    "STAT": ("sbuf", [128, 16], F32),
     "P0": ("sbuf", [128, 512], BF), "P1": ("sbuf", [128, 512], BF),
     "PT0": ("sbuf", [128, 512], BF), "PT1": ("sbuf", [128, 512], BF),
     "OA": ("sbuf", [128, 4 * MW], BF),
     "LT": ("sbuf", [128, 6 * MW], BF),
-    "ST": ("sbuf", [128, 32], F32), "NMIN": ("sbuf", [128, 4], F32), "W": ("sbuf", [128, 16], F32),
+    "NMIN": ("sbuf", [128, 4], F32), "W": ("sbuf", [128, 16], F32),
     "WL": ("sbuf", [128, 16], F32), "LS": ("sbuf", [128, 4], F32), "RL": ("sbuf", [128, 4], F32),
     "D": ("sbuf", [128, 2 * 3 * 128], BF),
     "YS": ("sbuf", [128, 4 * FD], BF),
@@ -180,21 +181,24 @@ def rank_program(g, core, T, topo):
     t_id = done("gp", g.affine_select(T.IDENT[:, :], T.ONES[:, :], [[-1, 128]], AluOpType.is_equal, 0.0, 0, 1))
 
     n = len(units)
-    tS, tMAX, tNG, tEXP, tT, tPTC, tPV, tEV = ([None] * n for _ in range(8))
+    tQ, tS, tMAX, tEXP, tPV, tEV, tST = ([None] * n for _ in range(7))
+    tT, tPTC = [[None, None] for _ in range(n)], [[None, None] for _ in range(n)]
 
-    def prev(lst, u):
-        return lst[u - 2] if u >= 2 else None
+    def prev(lst, u, d=2):
+        return lst[u - d] if u >= d else None
+
+    def stage_Q(u):
+        gi, jb = units[u]
+        need("ve", ("qa%d" % jb, qcount))
+        for slot in range(2):
+            c0 = (jb * 2 + slot) * HQ + gi * QP
+            tQ[u] = done("ve", g.vector.tensor_copy(T.QK[:, (2 * u + slot) * QP:(2 * u + slot + 1) * QP],
+                                                    T.QL[:, c0:c0 + QP]))
 
     def stage_S(u):
         gi, jb = units[u]
         h = HH * hh + gi
-        tqa = ("qa%d" % jb, qcount)
-        need("ve", tqa)
-        for slot in range(2):
-            c0 = (jb * 2 + slot) * HQ + gi * QP
-            tq = done("ve", g.vector.tensor_copy(T.QK[:, (2 * u + slot) * QP:(2 * u + slot + 1) * QP],
-                                                 T.QL[:, c0:c0 + QP]))
-        need("pe", tq, tqa, *kvdeps)
+        need("pe", tQ[u], ("qa%d" % jb, qcount), *kvdeps)
         need("pe", prev(tEXP, u), prev(tMAX, u))
         for kb in range(4):
             tS[u] = done("pe", g.tensor.matmul(Sps[u % 2][:, kb * 128:(kb + 1) * 128],
@@ -203,41 +207,49 @@ def rank_program(g, core, T, topo):
                                                start=True, stop=True))
 
     def stage_MAX(u):
-        gi, jb = units[u]
         need("ve", tS[u])
         tMAX[u] = done("ve", g.vector.tensor_reduce(T.NEGM[:, u:u + 1], Sps[u % 2][:, :], AxisListType.X,
                                                     AluOpType.max, negate=True))
-        need("ve", tMAX[u], t_pad)
-        for x in range(2):
-            base, src = (jb * 2 + x) * MW, T.NEGM[x * 64:(x + 1) * 64, u:u + 1]
-            if gi < 2:
-                c0 = base + FD + 1
-                tNG[u] = done("ve", g.vector.tensor_copy(T.OA[gi * 64:(gi + 1) * 64, c0:c0 + 1], src))
-            else:
-                c0 = base + BO[1] + BF_[1] + 1
-                done("ve", g.vector.tensor_copy(T.OA[0:64, c0:c0 + 1], src))
-                tNG[u] = done("ve", g.vector.tensor_copy(T.OA[64:128, c0:c0 + 1], src))
 
     def stage_EXP(u):
-        need("ac", tMAX[u], prev(tT, u), prev(tEV, u))
+        need("ac", tMAX[u], tT[u - 2][1] if u >= 2 else None)
         tEXP[u] = done("ac", g.scalar.activation(Pb[u % 2][:, :], Sps[u % 2][:, :], Exp,
                                                  bias=T.NEGM[:, u:u + 1], scale=1.0,
-                                                 accum_out=Ops[u % 2][:, FD:FD + 1]))
+                                                 accum_out=T.STAT[:, 2 * u:2 * u + 1]))
 
     def stage_T(u):
-        need("pe", tEXP[u], prev(tPTC, u), t_id)
-        for kb in range(4):
-            tT[u] = done("pe", g.tensor.transpose(PTP[u % 2][:, kb * 128:(kb + 1) * 128],
-                                                  Pb[u % 2][:, kb * 128:(kb + 1) * 128], T.IDENT[:, :]))
+        need("pe", tEXP[u], t_id)
+        for hf in range(2):
+            need("pe", tPTC[u - 1][hf] if u >= 1 else None)
+            for kb in (2 * hf, 2 * hf + 1):
+                tT[u][hf] = done("pe", g.tensor.transpose(PTP[hf][:, (kb % 2) * 128:(kb % 2 + 1) * 128],
+                                                          Pb[u % 2][:, kb * 128:(kb + 1) * 128], T.IDENT[:, :]))
 
     def stage_PTC(u):
-        need("ve", tT[u], prev(tPV, u))
-        tPTC[u] = done("ve", g.vector.tensor_copy(PTb[u % 2][:, :], PTP[u % 2][:, 0:512]))
+        for hf in range(2):
+            need("ve", tT[u][hf], prev(tPV, u))
+            tPTC[u][hf] = done("ve", g.vector.tensor_copy(PTb[u % 2][:, hf * 256:(hf + 1) * 256],
+                                                          PTP[hf][:, 0:256]))
+
+    def stage_ST(u):
+        gi, jb = units[u]
+        need("ve", tMAX[u])
+        t = done("ve", g.vector.tensor_copy(T.STAT[:, 2 * u + 1:2 * u + 2], T.NEGM[:, u:u + 1]))
+        need("ve", t, tEXP[u], t_pad)
+        for x in range(2):
+            base, src = (jb * 2 + x) * MW, T.STAT[x * 64:(x + 1) * 64, 2 * u:2 * u + 2]
+            if gi < 2:
+                tST[u] = done("ve", g.vector.tensor_copy(T.OA[gi * 64:(gi + 1) * 64, base + FD:base + FD + 2], src))
+            else:
+                c0 = base + BO[1] + BF_[1]
+                done("ve", g.vector.tensor_copy(T.OA[0:64, c0:c0 + 2], src))
+                tST[u] = done("ve", g.vector.tensor_copy(T.OA[64:128, c0:c0 + 2], src))
 
     def stage_PV(u):
         h = HH * hh + units[u][0]
-        need("pe", tPTC[u], prev(tEV, u), tEXP[u])
+        need("pe", prev(tEV, u))
         for kb in range(4):
+            need("pe", tPTC[u][kb // 2])
             tPV[u] = done("pe", g.tensor.matmul(Ops[u % 2][:, 0:FD], PTb[u % 2][:, kb * 128:(kb + 1) * 128],
                                                 T.VB[:, kb * NH * FD + h * FD: kb * NH * FD + (h + 1) * FD],
                                                 start=(kb == 0), stop=(kb == 3)))
@@ -245,29 +257,36 @@ def rank_program(g, core, T, topo):
     def stage_EV(u):
         gi, jb = units[u]
         ps = Ops[u % 2]
-        need("ac", tPV[u], tEXP[u], t_pad, t_ones)
+        need("ac", tPV[u], t_pad, t_ones)
         for x in range(2):
             base, r0, r1 = (jb * 2 + x) * MW, x * 64, (x + 1) * 64
             if gi < 2:
-                tEV[u] = done("ac", g.scalar.activation(T.OA[gi * 64:(gi + 1) * 64, base:base + FD + 1],
-                                                        ps[r0:r1, 0:FD + 1], Copy))
+                tEV[u] = done("ac", g.scalar.activation(T.OA[gi * 64:(gi + 1) * 64, base:base + FD],
+                                                        ps[r0:r1, 0:FD], Copy))
             else:
                 c0, hf = base + BO[1], BF_[1]
                 done("ac", g.scalar.activation(T.OA[0:64, c0:c0 + hf], ps[r0:r1, 0:hf], Copy))
-                done("ac", g.scalar.activation(T.OA[0:64, c0 + hf:c0 + hf + 1], ps[r0:r1, FD:FD + 1], Copy))
-                tEV[u] = done("ac", g.scalar.activation(T.OA[64:128, c0:c0 + hf + 1], ps[r0:r1, hf:FD + 1], Copy))
+                tEV[u] = done("ac", g.scalar.activation(T.OA[64:128, c0:c0 + hf], ps[r0:r1, hf:FD], Copy))
 
+    for u in range(n):
+        if units[u][1] == 0:
+            stage_Q(u)
     for u in range(min(2, n)):
         stage_S(u)
         stage_MAX(u)
         stage_EXP(u)
     for u in range(n):
+        if units[u][1] == 1:
+            stage_Q(u)
+    for u in range(n):
         stage_T(u)
         stage_PTC(u)
         if u + 2 < n:
             stage_S(u + 2)
-            stage_MAX(u + 2)
         stage_PV(u)
+        stage_ST(u)
+        if u + 2 < n:
+            stage_MAX(u + 2)
         stage_EV(u)
         if u + 2 < n:
             stage_EXP(u + 2)
@@ -279,7 +298,7 @@ def rank_program(g, core, T, topo):
         blk = gi - 1
         two, place = jobs[jb]
         es = engines(two)
-        need("gp", tEV[u], tNG[u], t_pad)
+        need("gp", tEV[u], tST[u], t_pad)
         fused([xfer(T.OA[:, (jb * 2 + x) * MW + BO[blk]:(jb * 2 + x) * MW + BO[blk] + BW[blk]],
                     T.LT[:, (place * 2 + hh) * MW + BO[blk]:(place * 2 + hh) * MW + BO[blk] + BW[blk]],
                     [two[x]], es[x * EO:(x + 1) * EO], "oa%d%d" % (hh, blk)) for x in range(2)])
@@ -288,17 +307,14 @@ def rank_program(g, core, T, topo):
         combos = [(0, 0), (1, 0), (0, 1), (1, 1)]
         tMM, tYE = [None] * 4, [None] * 4
         for k, (hx, blk) in enumerate(combos):
-            b, w0, d0, fw = k * 8, k * 4, (k % 2) * 384, BF_[blk]
+            w0, d0, fw = k * 4, (k % 2) * 384, BF_[blk]
             arr = ("oa%d%d" % (hx, blk), 3 * EO)
             cols = [(c * 2 + hx) * MW + BO[blk] for c in range(3)]
             need("ve", arr)
-            for c in range(3):
-                t = done("ve", g.vector.tensor_copy(T.ST[:, b + 2 * c:b + 2 * c + 2],
-                                                    T.LT[:, cols[c] + fw:cols[c] + fw + 2]))
-            need("ve", t)
-            sums, negs = T.ST[:, b:b + 5:2], T.ST[:, b + 1:b + 6:2]
+            sums = T.LT[:, cols[0] + fw:cols[2] + fw + 1:2 * MW]
+            negs = T.LT[:, cols[0] + fw + 1:cols[2] + fw + 2:2 * MW]
             t = done("ve", g.vector.tensor_reduce(T.NMIN[:, k:k + 1], negs, AxisListType.X, AluOpType.min))
-            need("ac", t)
+            need("ac", t, arr)
             t = done("ac", g.scalar.activation(T.W[:, w0:w0 + 3], negs, Exp, bias=T.NMIN[:, k:k + 1], scale=-1.0))
             need("ve", t, t_id, tMM[k - 2] if k >= 2 else None)
             for c in range(3):

@@ -24,8 +24,7 @@ SCRATCH = {
     "PT0": ("sbuf", [128, 512], BF), "PT1": ("sbuf", [128, 512], BF),
     "OA": ("sbuf", [128, 4 * MW], BF),
     "LT": ("sbuf", [128, 6 * MW], BF),
-    "NMIN": ("sbuf", [128, 4], F32), "W": ("sbuf", [128, 16], F32),
-    "WL": ("sbuf", [128, 16], F32), "LS": ("sbuf", [128, 4], F32), "RL": ("sbuf", [128, 4], F32),
+    "NMIN": ("sbuf", [128, 4], F32), "W": ("sbuf", [128, 16], F32), "RL": ("sbuf", [128, 4], F32),
     "D": ("sbuf", [128, 2 * 3 * 128], BF),
     "YS": ("sbuf", [128, 4 * FD], BF),
     "S0": ("psum", [128, 512], F32), "S1": ("psum", [128, 512], F32),
@@ -33,10 +32,10 @@ SCRATCH = {
     "O0": ("psum", [128, 512], F32), "O1": ("psum", [128, 512], F32),
     "Y0": ("psum", [128, 512], F32), "Y1": ("psum", [128, 512], F32),
 }
-SEMAPHORES = ["s_pe", "s_ve", "s_ac", "s_gp", "ld_q", "ld_kv0", "ld_kv1", "qa0", "qa1", "kv0", "kv1",
+SEMAPHORES = ["s_pe", "s_ve", "s_ac", "s_gp", "ld_q", "ld_k", "ld_v", "qa0", "qa1", "kk", "vv",
               "oa00", "oa01", "oa10", "oa11", "ls", "st"]
 
-EQ, EQH, EKV, EO = 4, 2, 4, 4
+EQ, EQH, EKV, EO = 4, 4, 8, 4
 
 
 def _layout(T, topo):
@@ -119,19 +118,19 @@ def rank_program(g, core, T, topo):
         hh = pos
         kcol = i * NH * KP
         g.sync.dma_start(T.QOWN[:, :], T.q[:, :]).then_inc(T.sem.ld_q, 16)
-        for half in range(2):
-            a, b = half * HH * KP, (half + 1) * HH * KP
-            g.sync.dma_start(T.KB[:, kcol + a:kcol + b], T.k[:, a:b]).then_inc(T.sem["ld_kv%d" % half], 16)
-            g.scalar.dma_start(T.VB[:, kcol + a:kcol + b], T.v[:, a:b]).then_inc(T.sem["ld_kv%d" % half], 16)
+        g.scalar.dma_start(T.KB[:, kcol:kcol + NH * KP], T.k[:, :]).then_inc(T.sem.ld_k, 16)
+        g.sync.dma_start(T.VB[:, kcol:kcol + NH * FD], T.v[:, :]).then_inc(T.sem.ld_v, 16)
         jobs = [(lay[chips[(ci + 1) % nch]][0][2 * pair:2 * pair + 2], 2),
                 (lay[chips[(ci + 2) % nch]][0][2 * pair:2 * pair + 2], 1)]
-        kvdeps = [("ld_kv%d" % hh, 32), ("kv%d" % hh, 3 * 2 * EKV)]
+        kdeps = [("ld_k", 16), ("kk", 3 * EKV)]
+        vdeps = [("ld_v", 16), ("vv", 3 * EKV)]
         units = [(0, 0), (1, 0), (0, 1), (1, 1), (2, 0), (2, 1)]
         qcount = 2 * EQ
     else:
         pair, hh = hpos[0]
         jobs = [(order[2 * pair:2 * pair + 2], 0)]
-        kvdeps = [("kv%d" % hh, 4 * 2 * EKV)]
+        kdeps = [("kk", 4 * EKV)]
+        vdeps = [("vv", 4 * EKV)]
         units = [(2, 0), (0, 0), (1, 0)]
         qcount = 2 * EQH
 
@@ -149,33 +148,33 @@ def rank_program(g, core, T, topo):
                 c0 = (jb * 2 + pos) * HQ
                 trs.append(xfer(T.QOWN[:, x * HQ:(x + 1) * HQ], T.QL[:, c0:c0 + HQ], [dst],
                                 eo[x * EQ:(x + 1) * EQ], "qa%d" % jb))
-            fused(trs)
+            return trs
 
-        def kv_out(to_ranks):
+        def kv_out(buf, sem, to_ranks):
             trs = []
             for x in range(2):
                 a, b = kcol + x * HH * KP, kcol + (x + 1) * HH * KP
                 if to_ranks:
                     dst = [order[2 * p + x] for p in range(len(helpers)) if order[2 * p + x] != core]
-                    ea = engines(dst)
-                    grp = [e for e in ea if (e in eo) == (x == pos)]
+                    grp = [e for e in engines(dst) if (e in eo) == (x == pos)]
                 else:
                     dst = [helpers[p][x] for p in range(len(helpers))]
-                    grp = engines(dst)[2 * x * EKV:(2 * x + 2) * EKV]
-                trs.append(xfer(T.KB[:, a:b], T.KB[:, a:b], dst, grp[0:EKV], "kv%d" % x))
-                trs.append(xfer(T.VB[:, a:b], T.VB[:, a:b], dst, grp[EKV:2 * EKV], "kv%d" % x))
+                    grp = engines(dst)[x * EKV:(x + 1) * EKV]
+                trs.append(xfer(buf[:, a:b], buf[:, a:b], dst, grp[0:EKV], sem))
             fused(trs)
 
         need("gp", ("ld_q", 16))
-        q_far(2, 0)
-        need("gp", ("ld_kv0", 32), ("ld_kv1", 32))
-        kv_out(True)
-        q_far(1, 1)
+        fused(q_far(2, 0))
+        need("gp", ("ld_k", 16))
+        kv_out(T.KB, "kk", True)
+        need("gp", ("ld_v", 16))
+        kv_out(T.VB, "vv", True)
         myh = helpers[pair]
-        eh = engines(myh)
-        fused([xfer(T.QOWN[:, x * HQ:(x + 1) * HQ], T.QL[:, pos * HQ:(pos + 1) * HQ],
-                    [myh[x]], eh[len(eh) - (x + 1) * EQH:len(eh) - x * EQH], "qa0") for x in range(2)])
-        kv_out(False)
+        eh = [e for e in engines(myh) if e not in eo]
+        fused(q_far(1, 1) + [xfer(T.QOWN[:, x * HQ:(x + 1) * HQ], T.QL[:, pos * HQ:(pos + 1) * HQ],
+                                  [myh[x]], eh[x * EQH:(x + 1) * EQH], "qa0") for x in range(2)])
+        kv_out(T.KB, "kk", False)
+        kv_out(T.VB, "vv", False)
 
     need("gp", t_ones)
     t_id = done("gp", g.affine_select(T.IDENT[:, :], T.ONES[:, :], [[-1, 128]], AluOpType.is_equal, 0.0, 0, 1))
@@ -198,7 +197,7 @@ def rank_program(g, core, T, topo):
     def stage_S(u):
         gi, jb = units[u]
         h = HH * hh + gi
-        need("pe", tQ[u], ("qa%d" % jb, qcount), *kvdeps)
+        need("pe", tQ[u], ("qa%d" % jb, qcount), *kdeps)
         need("pe", prev(tEXP, u), prev(tMAX, u))
         for kb in range(4):
             tS[u] = done("pe", g.tensor.matmul(Sps[u % 2][:, kb * 128:(kb + 1) * 128],
@@ -247,7 +246,7 @@ def rank_program(g, core, T, topo):
 
     def stage_PV(u):
         h = HH * hh + units[u][0]
-        need("pe", prev(tEV, u))
+        need("pe", prev(tEV, u), *vdeps)
         for kb in range(4):
             need("pe", tPTC[u][kb // 2])
             tPV[u] = done("pe", g.tensor.matmul(Ops[u % 2][:, 0:FD], PTb[u % 2][:, kb * 128:(kb + 1) * 128],
@@ -304,43 +303,52 @@ def rank_program(g, core, T, topo):
                     [two[x]], es[x * EO:(x + 1) * EO], "oa%d%d" % (hh, blk)) for x in range(2)])
 
     if is_rank:
-        combos = [(0, 0), (1, 0), (0, 1), (1, 1)]
         tMM, tYE = [None] * 4, [None] * 4
-        for k, (hx, blk) in enumerate(combos):
-            w0, d0, fw = k * 4, (k % 2) * 384, BF_[blk]
-            arr = ("oa%d%d" % (hx, blk), 3 * EO)
-            cols = [(c * 2 + hx) * MW + BO[blk] for c in range(3)]
-            need("ve", arr)
-            sums = T.LT[:, cols[0] + fw:cols[2] + fw + 1:2 * MW]
-            negs = T.LT[:, cols[0] + fw + 1:cols[2] + fw + 2:2 * MW]
-            t = done("ve", g.vector.tensor_reduce(T.NMIN[:, k:k + 1], negs, AxisListType.X, AluOpType.min))
-            need("ac", t, arr)
-            t = done("ac", g.scalar.activation(T.W[:, w0:w0 + 3], negs, Exp, bias=T.NMIN[:, k:k + 1], scale=-1.0))
-            need("ve", t, t_id, tMM[k - 2] if k >= 2 else None)
-            for c in range(3):
-                td = done("ve", g.vector.tensor_scalar(T.D[:, d0 + c * 128:d0 + (c + 1) * 128], T.IDENT[:, :],
-                                                       T.W[:, w0 + c:w0 + c + 1], None, AluOpType.mult))
-            t = done("ve", g.vector.tensor_tensor(T.WL[:, w0:w0 + 3], T.W[:, w0:w0 + 3], sums, AluOpType.mult))
-            need("ve", t)
-            t = done("ve", g.vector.tensor_reduce(T.LS[:, k:k + 1], T.WL[:, w0:w0 + 3], AxisListType.X,
-                                                  AluOpType.add))
-            need("ve", t)
-            trl = done("ve", g.vector.reciprocal(T.RL[:, k:k + 1], T.LS[:, k:k + 1]))
-
-            need("pe", td, arr, tYE[k - 2] if k >= 2 else None)
-            yp = Yps[k % 2]
-            for c in range(3):
-                tMM[k] = done("pe", g.tensor.matmul(yp[:, 0:fw], T.D[:, d0 + c * 128:d0 + (c + 1) * 128],
-                                                    T.LT[:, cols[c]:cols[c] + fw], start=(c == 0), stop=(c == 2)))
-            need("ac", tMM[k], trl)
-            tYE[k] = done("ac", g.scalar.activation(T.YS[:, k * FD:k * FD + fw], yp[:, 0:fw], Copy,
-                                                    scale=T.RL[:, k:k + 1]))
-            for lo, q in ((0, "sy"), (1, "ac")):
-                y0 = (HH * hx + lo) * FD if blk == 0 else (HH * hx + 2) * FD + lo * fw
-                need(q, tYE[k])
-                QUE[q].dma_start(T.y[:, y0:y0 + fw],
-                                 T.YS[lo * 64:(lo + 1) * 64, k * FD:k * FD + fw]).then_inc(T.sem.st, 16)
-                cnt["st"] += 16
+        for blk in range(2):
+            fw = BF_[blk]
+            ks = [2 * blk, 2 * blk + 1]
+            arr = {k: ("oa%d%d" % (k % 2, blk), 3 * EO) for k in ks}
+            cols = {k: [(c * 2 + k % 2) * MW + BO[blk] for c in range(3)] for k in ks}
+            negs = {k: T.LT[:, cols[k][0] + fw + 1:cols[k][2] + fw + 2:2 * MW] for k in ks}
+            tmin, tw, td, trl = {}, {}, {}, {}
+            for k in ks:
+                need("ve", arr[k])
+                tmin[k] = done("ve", g.vector.tensor_reduce(T.NMIN[:, k:k + 1], negs[k], AxisListType.X,
+                                                            AluOpType.min))
+            for k in ks:
+                need("ac", tmin[k], arr[k])
+                tw[k] = done("ac", g.scalar.activation(T.W[:, 4 * k:4 * k + 3], negs[k], Exp,
+                                                       bias=T.NMIN[:, k:k + 1], scale=-1.0))
+            for k in ks:
+                d0 = (k % 2) * 384
+                need("ve", tw[k], t_id, tMM[k - 2] if k >= 2 else None)
+                for c in range(3):
+                    td[k] = done("ve", g.vector.tensor_scalar(T.D[:, d0 + c * 128:d0 + (c + 1) * 128], T.IDENT[:, :],
+                                                              T.W[:, 4 * k + c:4 * k + c + 1], None, AluOpType.mult))
+            for k in ks:
+                d0 = (k % 2) * 384
+                need("pe", td[k], arr[k], tYE[k - 2] if k >= 2 else None)
+                for c in range(3):
+                    tMM[k] = done("pe", g.tensor.matmul(Yps[k % 2][:, 0:fw + 1],
+                                                        T.D[:, d0 + c * 128:d0 + (c + 1) * 128],
+                                                        T.LT[:, cols[k][c]:cols[k][c] + fw + 1],
+                                                        start=(c == 0), stop=(c == 2)))
+            for k in ks:
+                need("ve", tMM[k])
+                trl[k] = done("ve", g.vector.reciprocal(T.RL[:, k:k + 1], Yps[k % 2][:, fw:fw + 1]))
+            for k in ks:
+                need("ac", tMM[k], trl[k])
+                tYE[k] = done("ac", g.scalar.activation(T.YS[:, k * FD:k * FD + fw], Yps[k % 2][:, 0:fw], Copy,
+                                                        scale=T.RL[:, k:k + 1]))
+            for k in ks:
+                for lo in range(2):
+                    hx = k % 2
+                    y0 = (HH * hx + lo) * FD if blk == 0 else (HH * hx + 2) * FD + lo * fw
+                    q = "ac" if (hx == 1 and lo == 1) else "sy"
+                    need(q, tYE[k])
+                    QUE[q].dma_start(T.y[:, y0:y0 + fw],
+                                     T.YS[lo * 64:(lo + 1) * 64, k * FD:k * FD + fw]).then_inc(T.sem.st, 16)
+                    cnt["st"] += 16
 
     for name in ("s_pe", "s_ve", "s_ac", "s_gp", "ls", "st"):
         if cnt[name]:

from concourse.bass import DstId, RemoteDMATransfer
from concourse.mybir import AluOpType, AxisListType, ActivationFunctionType

NH, QP, KP, FD = 6, 64, 128, 128
HH = NH // 2
HQ = HH * QP
BW = (FD + 8, FD // 2 + 8)
BF_ = (FD, FD // 2)
BO = (0, FD + 8)
MW = BW[0] + BW[1]

BF, F32 = "bfloat16", "float32"
SCRATCH = {
    "QOWN": ("sbuf", [128, NH * QP], BF),
    "QL": ("sbuf", [128, 4 * HQ], BF),
    "QK": ("sbuf", [128, NH * 2 * QP], BF),
    "KB": ("sbuf", [128, 4 * NH * KP], BF),
    "VB": ("sbuf", [128, 4 * NH * FD], BF),
    "ONES": ("sbuf", [128, 128], BF),
    "IDENT": ("sbuf", [128, 128], BF),
    "NEGM": ("sbuf", [128, 8], BF),
    "STAT": ("sbuf", [128, 16], F32),
    "P0": ("sbuf", [128, 512], BF), "P1": ("sbuf", [128, 512], BF),
    "PT0": ("sbuf", [128, 512], BF), "PT1": ("sbuf", [128, 512], BF),
    "OA": ("sbuf", [128, 4 * MW], BF),
    "LT": ("sbuf", [128, 6 * MW], BF),
    "NMIN": ("sbuf", [128, 4], F32), "W": ("sbuf", [128, 16], F32), "RL": ("sbuf", [128, 4], F32),
    "D": ("sbuf", [128, 2 * 3 * 128], BF),
    "YS": ("sbuf", [128, 4 * FD], BF),
    "S0": ("psum", [128, 512], F32), "S1": ("psum", [128, 512], F32),
    "PTP0": ("psum", [128, 1024], BF), "PTP1": ("psum", [128, 1024], BF),
    "O0": ("psum", [128, 512], F32), "O1": ("psum", [128, 512], F32),
    "Y0": ("psum", [128, 512], F32), "Y1": ("psum", [128, 512], F32),
}
SEMAPHORES = ["s_pe", "s_ve", "s_ac", "s_gp", "ld_q", "ld_k", "ld_v", "qa0", "qa1", "kk", "vv",
              "oa00", "oa01", "oa10", "oa11", "ls", "st"]

EQ, EQH, EKV, EO = 4, 4, 8, 4


def _layout(T, topo):
    ranks = list(T.cores)
    chips = sorted({topo.chip(c) for c in ranks})
    ncores = topo.CHIPS * topo.CORES_PER_CHIP
    lay = {}
    for ch in chips:
        rs = [c for c in ranks if topo.chip(c) == ch]
        order, helpers = [], []
        for d in sorted({topo.die(c) for c in rs}):
            order += sorted(c for c in rs if topo.die(c) == d)
            helpers.append(sorted(c for c in range(ncores)
                                  if topo.chip(c) == ch and topo.die(c) == d and c not in ranks)[:2])
        lay[ch] = (order, helpers)
    return chips, lay


def rank_program(g, core, T, topo):
    chips, lay = _layout(T, topo)
    ch = topo.chip(core)
    if ch not in lay:
        return
    order, helpers = lay[ch]
    is_rank = core in order
    hpos = [(p, x) for p in range(len(helpers)) for x in range(2) if helpers[p][x] == core]
    if not is_rank and not hpos:
        return
    ci, nch = chips.index(ch), len(chips)

    Exp, Copy = ActivationFunctionType.Exp, ActivationFunctionType.Copy
    QUE = {"pe": g.tensor, "ve": g.vector, "ac": g.scalar, "gp": g, "sy": g.sync}
    ESEM = {"pe": "s_pe", "ve": "s_ve", "ac": "s_ac", "gp": "s_gp"}
    cnt = {"s_pe": 0, "s_ve": 0, "s_ac": 0, "s_gp": 0, "ls": 0, "st": 0}
    seen = {}

    def done(e, ins):
        name = ESEM[e]
        ins.then_inc(T.sem[name], 1)
        cnt[name] += 1
        return (name, cnt[name])

    def need(q, *toks):
        for t in toks:
            if t is None:
                continue
            name, n = t
            if seen.get((q, name), 0) < n:
                QUE[q].wait_ge(T.sem[name], n)
                seen[(q, name)] = n

    def engines(dsts):
        m = -1
        for d in dsts:
            assert topo.may_write(core, d)
            m &= topo.mask(core, d)
        return [e for e in range(64) if (m >> e) & 1]

    def xfer(src, dst_ap, dsts, engs, sem):
        ids = []
        for d in dsts:
            rid, pid, _se = topo.addr(d)
            ids.append(DstId(rid=rid, pnc=pid))
        m = 0
        for e in engs:
            m |= 1 << e
        cnt["ls"] += len(engs)
        return RemoteDMATransfer(dst_ids=ids, dma_engine_mask=m, remote_sem=T.sem[sem], srcs=[src],
                                 dsts=[dst_ap] * len(dsts), alu_op=0)

    def fused(trs):
        g.remote_dma_fused(trs, local_sem=T.sem.ls)

    Sps, PTP, Ops, Yps = [T.S0, T.S1], [T.PTP0, T.PTP1], [T.O0, T.O1], [T.Y0, T.Y1]
    Pb, PTb = [T.P0, T.P1], [T.PT0, T.PT1]

    if is_rank:
        i = order.index(core)
        pair, pos = i // 2, i % 2
        hh = pos
        kcol = i * NH * KP
        g.sync.dma_start(T.QOWN[:, :], T.q[:, :]).then_inc(T.sem.ld_q, 16)
        g.scalar.dma_start(T.KB[:, kcol:kcol + NH * KP], T.k[:, :]).then_inc(T.sem.ld_k, 16)
        g.sync.dma_start(T.VB[:, kcol:kcol + NH * FD], T.v[:, :]).then_inc(T.sem.ld_v, 16)
        jobs = [(lay[chips[(ci + 1) % nch]][0][2 * pair:2 * pair + 2], 2),
                (lay[chips[(ci + 2) % nch]][0][2 * pair:2 * pair + 2], 1)]
        kdeps = [("ld_k", 16), ("kk", 3 * EKV)]
        vdeps = [("ld_v", 16), ("vv", 3 * EKV)]
        units = [(0, 0), (1, 0), (0, 1), (1, 1), (2, 0), (2, 1)]
        qcount = 2 * EQ
    else:
        pair, hh = hpos[0]
        jobs = [(order[2 * pair:2 * pair + 2], 0)]
        kdeps = [("kk", 4 * EKV)]
        vdeps = [("vv", 4 * EKV)]
        units = [(2, 0), (0, 0), (1, 0)]
        qcount = 2 * EQH

    t_pad = done("ve", g.vector.memset(T.OA[:, :], 0.0))
    need("ac", t_pad)
    t_ones = done("ac", g.scalar.activation(T.ONES[:, :], T.OA[:, 0:128], Exp))

    if is_rank:
        eo = engines([lay[chips[(ci + s) % nch]][0][2 * pair + x] for s in (1, 2) for x in range(2)])

        def q_far(s, jb):
            trs = []
            for x in range(2):
                dst = lay[chips[(ci + s) % nch]][0][2 * pair + x]
                c0 = (jb * 2 + pos) * HQ
                trs.append(xfer(T.QOWN[:, x * HQ:(x + 1) * HQ], T.QL[:, c0:c0 + HQ], [dst],
                                eo[x * EQ:(x + 1) * EQ], "qa%d" % jb))
            return trs

        def kv_out(buf, sem, to_ranks):
            trs = []
            for x in range(2):
                a, b = kcol + x * HH * KP, kcol + (x + 1) * HH * KP
                if to_ranks:
                    dst = [order[2 * p + x] for p in range(len(helpers)) if order[2 * p + x] != core]
                    grp = [e for e in engines(dst) if (e in eo) == (x == pos)]
                else:
                    dst = [helpers[p][x] for p in range(len(helpers))]
                    grp = engines(dst)[x * EKV:(x + 1) * EKV]
                trs.append(xfer(buf[:, a:b], buf[:, a:b], dst, grp[0:EKV], sem))
            fused(trs)

        need("gp", ("ld_q", 16))
        fused(q_far(2, 0))
        need("gp", ("ld_k", 16))
        kv_out(T.KB, "kk", True)
        need("gp", ("ld_v", 16))
        kv_out(T.VB, "vv", True)
        myh = helpers[pair]
        eh = [e for e in engines(myh) if e not in eo]
        fused(q_far(1, 1) + [xfer(T.QOWN[:, x * HQ:(x + 1) * HQ], T.QL[:, pos * HQ:(pos + 1) * HQ],
                                  [myh[x]], eh[x * EQH:(x + 1) * EQH], "qa0") for x in range(2)])
        kv_out(T.KB, "kk", False)
        kv_out(T.VB, "vv", False)

    need("gp", t_ones)
    t_id = done("gp", g.affine_select(T.IDENT[:, :], T.ONES[:, :], [[-1, 128]], AluOpType.is_equal, 0.0, 0, 1))

    n = len(units)
    tQ, tS, tMAX, tEXP, tPV, tEV, tST = ([None] * n for _ in range(7))
    tT, tPTC = [[None, None] for _ in range(n)], [[None, None] for _ in range(n)]

    def prev(lst, u, d=2):
        return lst[u - d] if u >= d else None

    def stage_Q(u):
        gi, jb = units[u]
        need("ve", ("qa%d" % jb, qcount))
        for slot in range(2):
            c0 = (jb * 2 + slot) * HQ + gi * QP
            tQ[u] = done("ve", g.vector.tensor_copy(T.QK[:, (2 * u + slot) * QP:(2 * u + slot + 1) * QP],
                                                    T.QL[:, c0:c0 + QP]))

    def stage_S(u):
        gi, jb = units[u]
        h = HH * hh + gi
        need("pe", tQ[u], ("qa%d" % jb, qcount), *kdeps)
        need("pe", prev(tEXP, u), prev(tMAX, u))
        for kb in range(4):
            tS[u] = done("pe", g.tensor.matmul(Sps[u % 2][:, kb * 128:(kb + 1) * 128],
                                               T.QK[:, 2 * u * QP:(2 * u + 2) * QP],
                                               T.KB[:, kb * NH * KP + h * KP: kb * NH * KP + (h + 1) * KP],
                                               start=True, stop=True))

    def stage_MAX(u):
        need("ve", tS[u])
        tMAX[u] = done("ve", g.vector.tensor_reduce(T.NEGM[:, u:u + 1], Sps[u % 2][:, :], AxisListType.X,
                                                    AluOpType.max, negate=True))

    def stage_EXP(u):
        need("ac", tMAX[u], tT[u - 2][1] if u >= 2 else None)
        tEXP[u] = done("ac", g.scalar.activation(Pb[u % 2][:, :], Sps[u % 2][:, :], Exp,
                                                 bias=T.NEGM[:, u:u + 1], scale=1.0,
                                                 accum_out=T.STAT[:, 2 * u:2 * u + 1]))

    def stage_T(u):
        need("pe", tEXP[u], t_id)
        for hf in range(2):
            need("pe", tPTC[u - 1][hf] if u >= 1 else None)
            for kb in (2 * hf, 2 * hf + 1):
                tT[u][hf] = done("pe", g.tensor.transpose(PTP[hf][:, (kb % 2) * 128:(kb % 2 + 1) * 128],
                                                          Pb[u % 2][:, kb * 128:(kb + 1) * 128], T.IDENT[:, :]))

    def stage_PTC(u):
        for hf in range(2):
            need("ve", tT[u][hf], prev(tPV, u))
            tPTC[u][hf] = done("ve", g.vector.tensor_copy(PTb[u % 2][:, hf * 256:(hf + 1) * 256],
                                                          PTP[hf][:, 0:256]))

    def stage_ST(u):
        gi, jb = units[u]
        need("ve", tMAX[u])
        t = done("ve", g.vector.tensor_copy(T.STAT[:, 2 * u + 1:2 * u + 2], T.NEGM[:, u:u + 1]))
        need("ve", t, tEXP[u], t_pad)
        for x in range(2):
            base, src = (jb * 2 + x) * MW, T.STAT[x * 64:(x + 1) * 64, 2 * u:2 * u + 2]
            if gi < 2:
                tST[u] = done("ve", g.vector.tensor_copy(T.OA[gi * 64:(gi + 1) * 64, base + FD:base + FD + 2], src))
            else:
                c0 = base + BO[1] + BF_[1]
                done("ve", g.vector.tensor_copy(T.OA[0:64, c0:c0 + 2], src))
                tST[u] = done("ve", g.vector.tensor_copy(T.OA[64:128, c0:c0 + 2], src))

    def stage_PV(u):
        h = HH * hh + units[u][0]
        need("pe", prev(tEV, u), *vdeps)
        for kb in range(4):
            need("pe", tPTC[u][kb // 2])
            tPV[u] = done("pe", g.tensor.matmul(Ops[u % 2][:, 0:FD], PTb[u % 2][:, kb * 128:(kb + 1) * 128],
                                                T.VB[:, kb * NH * FD + h * FD: kb * NH * FD + (h + 1) * FD],
                                                start=(kb == 0), stop=(kb == 3)))

    def stage_EV(u):
        gi, jb = units[u]
        ps = Ops[u % 2]
        need("ac", tPV[u], t_pad, t_ones)
        for x in range(2):
            base, r0, r1 = (jb * 2 + x) * MW, x * 64, (x + 1) * 64
            if gi < 2:
                tEV[u] = done("ac", g.scalar.activation(T.OA[gi * 64:(gi + 1) * 64, base:base + FD],
                                                        ps[r0:r1, 0:FD], Copy))
            else:
                c0, hf = base + BO[1], BF_[1]
                done("ac", g.scalar.activation(T.OA[0:64, c0:c0 + hf], ps[r0:r1, 0:hf], Copy))
                tEV[u] = done("ac", g.scalar.activation(T.OA[64:128, c0:c0 + hf], ps[r0:r1, hf:FD], Copy))

    for u in range(n):
        if units[u][1] == 0:
            stage_Q(u)
    for u in range(min(2, n)):
        stage_S(u)
        stage_MAX(u)
        stage_EXP(u)
    for u in range(n):
        if units[u][1] == 1:
            stage_Q(u)
    for u in range(n):
        stage_T(u)
        stage_PTC(u)
        if u + 2 < n:
            stage_S(u + 2)
        stage_PV(u)
        stage_ST(u)
        if u + 2 < n:
            stage_MAX(u + 2)
        stage_EV(u)
        if u + 2 < n:
            stage_EXP(u + 2)

    for u in range(n):
        gi, jb = units[u]
        if gi == 0:
            continue
        blk = gi - 1
        two, place = jobs[jb]
        es = engines(two)
        need("gp", tEV[u], tST[u], t_pad)
        fused([xfer(T.OA[:, (jb * 2 + x) * MW + BO[blk]:(jb * 2 + x) * MW + BO[blk] + BW[blk]],
                    T.LT[:, (place * 2 + hh) * MW + BO[blk]:(place * 2 + hh) * MW + BO[blk] + BW[blk]],
                    [two[x]], es[x * EO:(x + 1) * EO], "oa%d%d" % (hh, blk)) for x in range(2)])

    if is_rank:
        tMM, tYE = [None] * 4, [None] * 4
        for blk in range(2):
            fw = BF_[blk]
            ks = [2 * blk, 2 * blk + 1]
            arr = {k: ("oa%d%d" % (k % 2, blk), 3 * EO) for k in ks}
            cols = {k: [(c * 2 + k % 2) * MW + BO[blk] for c in range(3)] for k in ks}
            negs = {k: T.LT[:, cols[k][0] + fw + 1:cols[k][2] + fw + 2:2 * MW] for k in ks}
            tmin, tw, td, trl = {}, {}, {}, {}
            for k in ks:
                need("ve", arr[k])
                tmin[k] = done("ve", g.vector.tensor_reduce(T.NMIN[:, k:k + 1], negs[k], AxisListType.X,
                                                            AluOpType.min))
            for k in ks:
                need("ac", tmin[k], arr[k])
                tw[k] = done("ac", g.scalar.activation(T.W[:, 4 * k:4 * k + 3], negs[k], Exp,
                                                       bias=T.NMIN[:, k:k + 1], scale=-1.0))
            for k in ks:
                d0 = (k % 2) * 384
                need("ve", tw[k], t_id, tMM[k - 2] if k >= 2 else None)
                for c in range(3):
                    td[k] = done("ve", g.vector.tensor_scalar(T.D[:, d0 + c * 128:d0 + (c + 1) * 128], T.IDENT[:, :],
                                                              T.W[:, 4 * k + c:4 * k + c + 1], None, AluOpType.mult))
            for k in ks:
                d0 = (k % 2) * 384
                need("pe", td[k], arr[k], tYE[k - 2] if k >= 2 else None)
                for c in range(3):
                    tMM[k] = done("pe", g.tensor.matmul(Yps[k % 2][:, 0:fw + 1],
                                                        T.D[:, d0 + c * 128:d0 + (c + 1) * 128],
                                                        T.LT[:, cols[k][c]:cols[k][c] + fw + 1],
                                                        start=(c == 0), stop=(c == 2)))
            for k in ks:
                need("ve", tMM[k])
                trl[k] = done("ve", g.vector.reciprocal(T.RL[:, k:k + 1], Yps[k % 2][:, fw:fw + 1]))
            for k in ks:
                need("ac", tMM[k], trl[k])
                tYE[k] = done("ac", g.scalar.activation(T.YS[:, k * FD:k * FD + fw], Yps[k % 2][:, 0:fw], Copy,
                                                        scale=T.RL[:, k:k + 1]))
            for k in ks:
                for lo in range(2):
                    hx = k % 2
                    y0 = (HH * hx + lo) * FD if blk == 0 else (HH * hx + 2) * FD + lo * fw
                    q = "ac" if (hx == 1 and lo == 1) else "sy"
                    need(q, tYE[k])
                    QUE[q].dma_start(T.y[:, y0:y0 + fw],
                                     T.YS[lo * 64:(lo + 1) * 64, k * FD:k * FD + fw]).then_inc(T.sem.st, 16)
                    cnt["st"] += 16

    for name in ("s_pe", "s_ve", "s_ac", "s_gp", "ls", "st"):
        if cnt[name]:
            need("gp", (name, cnt[name]))
